import numpy as np
import ml_dtypes


def mxq(x, axis, fmt="e4m3"):
    dtype, down = {"e4m3": (ml_dtypes.float8_e4m3fn, 7), "e5m2": (ml_dtypes.float8_e5m2, 14)}[fmt]
    v = np.moveaxis(np.asarray(x, np.float32).astype(ml_dtypes.bfloat16).astype(np.float64), axis, -1)
    blocks = v.reshape(v.shape[:-1] + (-1, 32))
    amax = np.abs(blocks).max(-1, keepdims=True)
    byte = np.maximum(np.where(amax > 0, np.frexp(amax)[1] - 1 + 127, 0) - down, 1)
    scale = np.exp2(byte - 127.0)
    codes = (blocks / scale).astype(np.float32).astype(dtype).astype(np.float64)
    return np.moveaxis((codes * scale).reshape(v.shape), -1, axis)


WIDE = False


def mx_kscale(k):
    if not WIDE:
        return np.ones(k)
    levels = np.array([30, -30])
    if k % 512:
        return np.exp2(np.random.permutation(np.resize(levels, k // 32))).repeat(32)
    a = np.empty((k // 512, 16))
    for p in range(k // 512):
        a[p, :8] = np.random.permutation(np.resize(levels, 8))
        for g in range(8):
            far = levels[np.abs(levels - a[p, g]) >= 10]
            a[p, g + 8] = far[np.random.randint(len(far))]
    return np.exp2(a.ravel()).repeat(32)


def f64(x):
    return np.asarray(x).astype(np.float64)


def striped(idx):
    return np.tile(np.asarray(idx).reshape(-1, 16).T, (8, 1)).astype(np.uint16)


def unstriped(offs):
    return offs[:16].T.reshape(-1).astype(np.int64)


def striped8(idx):
    return np.asarray(idx).reshape(8, -1, 16).transpose(0, 2, 1).reshape(128, -1).astype(np.uint16)


def unstriped8(offs):
    return offs.reshape(8, 16, -1).transpose(0, 2, 1).reshape(8, -1).astype(np.int64)


def pick8(x, idx, run):
    r = np.arange(len(x))
    return x[r[:, None], idx[r % (8 * run) // run]]


def bf(x):
    return np.asarray(x, np.float32).astype(ml_dtypes.bfloat16)


def planes(Y):
    r, m = Y.shape
    b = f64(bf(Y)).reshape(r // 32, 32, m)
    amax = np.abs(b).max(1)
    byte = np.clip(np.where(amax > 0, np.frexp(amax)[1] - 1 + 127 - 7, 1), 1, 254)
    codes = (b * np.exp2(127.0 - byte)[:, None, :]).reshape(r, m).astype(np.float32).astype(ml_dtypes.float8_e4m3fn).view(np.uint8)
    words = codes.reshape(r // 512, 128, 4, m).transpose(0, 1, 3, 2)
    return np.ascontiguousarray(words), np.ascontiguousarray(byte.astype(np.uint8).reshape(r // 512, 16, m))


K, J, N, T, V = 512, 512, 256, 1024, 1024


def setup_inputs():
    n = np.random.standard_normal
    idx = np.stack([np.random.permutation(T)[:J] for _ in range(8)])
    idx2 = np.random.permutation(V)[:J]
    fj = mx_kscale(J)
    return {
        "xf": (n((K, T))).astype(np.float32),
        "ra": (np.random.uniform(0.5, 1.5, (1, J)) * fj).astype(np.float32),
        "gt": (n((N, V)) * np.exp(0.5 * n((1, V)))).astype(np.float32),
        "rb": (np.random.uniform(0.5, 1.5, (1, J)) / fj).astype(np.float32),
        "cp": (np.random.uniform(0.4, 1.2, (N, 1))).astype(np.float32),
        "old": (12.0 * n((K, N))).astype(np.float32),
        "offs": striped8(idx),
        "offs2": striped(idx2),
    }


def reference(xf, ra, gt, rb, cp, old, offs, offs2):
    idx = unstriped8(offs)
    idx2 = unstriped(offs2)
    us = pick8(f64(xf), idx, 64) * f64(ra)
    uj = us.T
    gs = np.minimum(f64(gt)[:, idx2], f64(cp)) * f64(rb)
    gj = gs.T
    ujq = mxq(uj, 0, "e5m2")
    gjq = mxq(gj, 0, "e5m2")
    w = ujq.T @ gjq
    y = 0.04 * np.maximum(w, f64(old))
    words, scales = planes(y)
    return y, words, scales

@@ -1,0 +1,175 @@
+from contextlib import ExitStack
+
+import concourse.mybir as mybir
+from concourse.masks import make_identity
+
+K, J, N, T, V = 512, 512, 256, 1024, 1024
+FLOPS = 2 * K * J * N
+
+F32 = mybir.dt.float32
+BF16 = mybir.dt.bfloat16
+I32 = mybir.dt.int32
+U32 = mybir.dt.uint32
+U16 = mybir.dt.uint16
+U8 = mybir.dt.uint8
+E5M2X4 = mybir.dt.float8_e5m2_x4
+E4M3X4 = mybir.dt.float8_e4m3fn_x4
+COPY = mybir.ActivationFunctionType.Copy
+ALU = mybir.AluOpType
+
+P = 128
+PACK = 4
+HALVES = N // P
+GAIN = 0.04
+X_GATHER = [[["S",0,256],["V",256,512]],[["S",0,256],["V",256,512]],[["S",0,256],["V",256,512]],[["S",0,256],["S",256,512]]]
+G_GATHER = [[["S",0,384],["V",384,512]],[["S",0,384],["V",384,512]]]
+X_MULT = [[[0,512]],[[0,512]],[[0,512]],[[0,256],[256,512]]]
+X_GROUPS = [[0,1],[2],[3]]
+
+
+def tile_list_moment_headpicks_bounded_larger_pl_kernel(tc, xf, ra, gt, rb, cp, old, offs, offs2, out_0, out_1, out_2):
+    nc = tc.nc
+    with ExitStack() as ctx:
+        keep = ctx.enter_context(tc.tile_pool(name="keep", bufs=1))
+        psum = ctx.enter_context(tc.psum_pool(name="psum", bufs=1))
+
+        x_list = keep.tile([P, J // 16], U16, name="x_list")
+        g_list = keep.tile([P, J // 16], U16, name="g_list")
+        x_win = [keep.tile([P, T], F32, name="x_win%d" % t) for t in range(PACK)]
+        g_win = [keep.tile([P, V], F32, name="g_win%d" % h) for h in range(HALVES)]
+        ra4 = keep.tile([P, PACK], F32, name="ra4")
+        rb4 = keep.tile([P, PACK], F32, name="rb4")
+        bound = [keep.tile([P, 1], F32, name="bound%d" % h) for h in range(HALVES)]
+        old_sb = keep.tile([P, PACK, N], F32, name="old_sb")
+        x_rows = xf.rearrange("(p t) c -> p t c", t=PACK)
+
+        nc.sync.dma_start(g_win[0][:], gt[0:P, :])
+        nc.sync.dma_start(g_list[:], offs2)
+        nc.scalar.dma_start(rb4[:], rb.rearrange("o (q i) -> q (o i)", i=PACK))
+        nc.scalar.dma_start(bound[0][:], cp[0:P, :])
+        nc.scalar.dma_start(ra4[:], ra.rearrange("o (q i) -> q (o i)", i=PACK))
+        nc.sync.dma_start(g_win[1][:], gt[P : 2 * P, :])
+        nc.sync.dma_start(bound[1][:], cp[P : 2 * P, :])
+        nc.sync.dma_start(x_win[0][:], x_rows[:, 0, :])
+        nc.sync.dma_start(x_list[:], offs)
+        nc.sync.dma_start(x_win[1][:], x_rows[:, 1, :])
+        nc.sync.dma_start(x_win[2][:], x_rows[:, 2, :])
+        nc.sync.dma_start(x_win[3][:], x_rows[:, 3, :])
+        nc.sync.dma_start(old_sb[:], old.rearrange("(p t) n -> p t n", t=PACK))
+
+        ident = keep.tile([P, P], F32, name="ident")
+        zero = keep.tile([P, 1], F32, name="zero")
+        nc.gpsimd.memset(zero[:], 0.0)
+        nc.scalar.activation(ident[:], zero[:].to_broadcast([P, P]), COPY)
+        make_identity(nc, ident[:], nomemset=True)
+
+        def spread(name, column4):
+            everywhere = psum.tile([P, PACK, P], F32, name=name)
+            for i in range(PACK):
+                nc.tensor.transpose(everywhere[:, i, :], column4[:, i : i + 1].to_broadcast([P, P]), ident[:])
+            return everywhere
+
+        def gather(name, window, offsets, pieces):
+            picked = keep.tile([P, J], F32, name=name)
+            for engine, first, last in pieces:
+                listed = window[:].indirect(offsets[:, first // 16 : last // 16])
+                if engine == "S":
+                    nc.scalar.activation(picked[:, first:last], listed, COPY)
+                else:
+                    nc.vector.tensor_copy(picked[:, first:last], listed)
+            return picked[:].rearrange("p (q u e) -> p u q e", u=2, e=2)
+
+        def turn(rounded, turned):
+            for u in range(2):
+                nc.tensor.transpose(turned[:, u, :], rounded[:, u, :].bitcast(F32), ident[:])
+
+        def quantise(name, turned, count, copy):
+            grouped = keep.tile([P, count * P * PACK], BF16, name=name + "_grouped", align_bytes=64)
+            words = keep.tile([P, count * P], U32, name=name + "_words", align_bytes=64)
+            scales = keep.tile([P, count * P], U8, name=name + "_scales", align_bytes=64)
+            copy(grouped[:].bitcast(F32).rearrange("q (a c u) -> q a c u", a=count, u=2), turned[:].rearrange("q a u c -> q a c u"))
+            nc.vector.quantize_mx(out=words[:].bitcast(E5M2X4), scales=scales[:], in_=grouped[:])
+            return words, scales
+
+        rb_all = spread("rb_all", rb4)
+        g_turned = psum.tile([P, HALVES, 2, P], F32, name="g_turned", tag="turned0")
+        for h in range(HALVES):
+            picked = gather("g_picked%d" % h, g_win[h], g_list, G_GATHER[h])
+            rounded = keep.tile([P, 2, 2 * P], BF16, name="g_rounded%d" % h, align_bytes=64)
+            for u in range(2):
+                nc.vector.scalar_tensor_tensor(
+                    rounded[:, u, :].rearrange("p (q e) -> p q e", e=2),
+                    picked[:, u, :, :],
+                    bound[h][:],
+                    rb_all[:, 2 * u : 2 * u + 2, :].rearrange("p e q -> p q e"),
+                    ALU.min,
+                    ALU.mult,
+                )
+            turn(rounded, g_turned[:, h, :, :])
+        g_words, g_scales = quantise("g", g_turned, HALVES, nc.scalar.copy)
+
+        ra_all = spread("ra_all", ra4)
+        acc01 = psum.tile([P, 2, N], F32, name="acc01")
+        acc2 = psum.tile([P, N], F32, name="acc2")
+        acc3 = [psum.tile([P, P], F32, name="acc3%d" % h, tag=["acc30", "rb_all"][h]) for h in range(HALVES)]
+        for group, (planes, copy) in enumerate(zip(X_GROUPS, [nc.scalar.copy, nc.scalar.copy, nc.scalar.copy])):
+            x_turned = psum.tile([P, len(planes), 2, P], F32, name="x_turned%d" % group, tag="turned%d" % ((group + 1) % 2))
+            for a, t in enumerate(planes):
+                picked = gather("x_picked%d" % t, x_win[t], x_list, X_GATHER[t])
+                rounded = keep.tile([P, 2, 2 * P], BF16, name="x_rounded%d" % t, align_bytes=64)
+                for first, last in X_MULT[t]:
+                    part = slice(first // PACK, last // PACK)
+                    nc.vector.tensor_tensor(
+                        rounded[:].rearrange("p u (q e) -> p u q e", e=2)[:, :, part, :],
+                        picked[:, :, part, :],
+                        ra_all[:, :, part].rearrange("p (u e) q -> p u q e", e=2),
+                        ALU.mult,
+                    )
+                turn(rounded, x_turned[:, a, :, :])
+            x_words, x_scales = quantise("x%d" % group, x_turned, len(planes), copy)
+            for a, t in enumerate(planes):
+                mine = slice(a * P, (a + 1) * P)
+                if t < 3:
+                    targets = [(acc01[:, t, :] if t < 2 else acc2[:], slice(0, N))]
+                else:
+                    targets = [(acc3[h][:], slice(h * P, (h + 1) * P)) for h in range(HALVES)]
+                for target, cols in targets:
+                    nc.tensor.matmul_mx(
+                        out=target,
+                        lhsT=x_words[:, mine].bitcast(E5M2X4),
+                        lhsT_scale=x_scales[:, mine],
+                        rhs=g_words[:, cols].bitcast(E5M2X4),
+                        rhs_scale=g_scales[:, cols],
+                        start=True,
+                        stop=True,
+                    )
+
+        y_rows = out_0.rearrange("(p t) n -> p t n", t=PACK)
+        word_rows = out_1.rearrange("z p c r -> p (z c r)").bitcast(I32)
+        scale_rows = out_2.rearrange("z q c -> q (z c)").bitcast(I32)
+        larger = keep.tile([P, PACK, N], F32, name="larger")
+        y = keep.tile([P, PACK, N], F32, name="y")
+        y_words = keep.tile([P, N], U32, name="y_words", align_bytes=64)
+        y_scales = keep.tile([P, N], U8, name="y_scales", align_bytes=64)
+        y_grouped = keep.tile([P, N, PACK], BF16, name="y_grouped", align_bytes=64)
+        nc.vector.tensor_tensor(larger[:, 0:2, :], acc01[:], old_sb[:, 0:2, :], ALU.max)
+
+        nc.vector.tensor_tensor(larger[:, 2, :], acc2[:], old_sb[:, 2, :], ALU.max)
+        for h in range(HALVES):
+            cols = slice(h * P, (h + 1) * P)
+            nc.vector.tensor_tensor(larger[:, 3, cols], acc3[h][:], old_sb[:, 3, cols], ALU.max)
+        for rows in (slice(0, 2), slice(2, PACK)):
+            nc.scalar.activation(y[:, rows, :], larger[:, rows, :], COPY, scale=GAIN)
+            nc.sync.dma_start(y_rows[:, rows, :], y[:, rows, :])
+        for h in range(HALVES):
+            cols = slice(h * P, (h + 1) * P)
+            nc.vector.tensor_scalar(y_grouped[:, cols, 0:PACK], larger[:, 0:PACK, cols].rearrange("p t c -> p c t"), GAIN, None, ALU.mult)
+        for h in range(HALVES):
+            cols = slice(h * P, (h + 1) * P)
+            nc.vector.quantize_mx(
+                out=y_words[:, cols].bitcast(E4M3X4), scales=y_scales[:, cols], in_=y_grouped[:, cols, :].rearrange("p c t -> p (c t)")
+            )
+        nc.sync.dma_start(word_rows, y_words[:].bitcast(I32))
+        for quad in range(4):
+            queue = nc.scalar if quad % 2 == 0 else nc.sync
+            queue.dma_start(scale_rows[4 * quad : 4 * quad + 4, :], y_scales[32 * quad : 32 * quad + 4, :].bitcast(I32))

@@ -21,10 +21,10 @@ P = 128
 PACK = 4
 HALVES = N // P
 GAIN = 0.04
-X_GATHER = [[["S",0,256],["V",256,512]],[["S",0,256],["V",256,512]],[["S",0,256],["V",256,512]],[["S",0,256],["S",256,512]]]
-G_GATHER = [[["S",0,384],["V",384,512]],[["S",0,384],["V",384,512]]]
+X_GATHER = [[["S",0,512]],[["S",0,512]],[["S",0,512]],[["S",0,256],["S",256,512]]]
+G_GATHER = [[["S",0,512]],[["S",0,512]]]
 X_MULT = [[[0,512]],[[0,512]],[[0,512]],[[0,256],[256,512]]]
-X_GROUPS = [[0,1],[2],[3]]
+X_GROUPS = [[0],[1],[2],[3]]
 
 
 def tile_list_moment_headpicks_bounded_larger_pl_kernel(tc, xf, ra, gt, rb, cp, old, offs, offs2, out_0, out_1, out_2):
@@ -83,17 +83,16 @@ def tile_list_moment_headpicks_bounded_larger_pl_kernel(tc, xf, ra, gt, rb, cp, 
             for u in range(2):
                 nc.tensor.transpose(turned[:, u, :], rounded[:, u, :].bitcast(F32), ident[:])
 
-        def quantise(name, turned, count, copy):
+        def quantise(name, turned, count, copy, words, scales):
             grouped = keep.tile([P, count * P * PACK], BF16, name=name + "_grouped", align_bytes=64)
-            words = keep.tile([P, count * P], U32, name=name + "_words", align_bytes=64)
-            scales = keep.tile([P, count * P], U8, name=name + "_scales", align_bytes=64)
             copy(grouped[:].bitcast(F32).rearrange("q (a c u) -> q a c u", a=count, u=2), turned[:].rearrange("q a u c -> q a c u"))
-            nc.vector.quantize_mx(out=words[:].bitcast(E5M2X4), scales=scales[:], in_=grouped[:])
-            return words, scales
+            nc.vector.quantize_mx(out=words.bitcast(E5M2X4), scales=scales, in_=grouped[:])
 
         rb_all = spread("rb_all", rb4)
-        g_turned = psum.tile([P, HALVES, 2, P], F32, name="g_turned", tag="turned0")
+        g_words = keep.tile([P, N], U32, name="g_words", align_bytes=64)
+        g_scales = keep.tile([P, N], U8, name="g_scales", align_bytes=64)
         for h in range(HALVES):
+            g_turned = psum.tile([P, 1, 2, P], F32, name="g_turned%d" % h, tag="turned%d" % h)
             picked = gather("g_picked%d" % h, g_win[h], g_list, G_GATHER[h])
             rounded = keep.tile([P, 2, 2 * P], BF16, name="g_rounded%d" % h, align_bytes=64)
             for u in range(2):
@@ -105,15 +104,15 @@ def tile_list_moment_headpicks_bounded_larger_pl_kernel(tc, xf, ra, gt, rb, cp, 
                     ALU.min,
                     ALU.mult,
                 )
-            turn(rounded, g_turned[:, h, :, :])
-        g_words, g_scales = quantise("g", g_turned, HALVES, nc.scalar.copy)
+            turn(rounded, g_turned[:, 0, :, :])
+            quantise("g%d" % h, g_turned, 1, nc.vector.tensor_copy, g_words[:, h * P : (h + 1) * P], g_scales[:, h * P : (h + 1) * P])
 
         ra_all = spread("ra_all", ra4)
         acc01 = psum.tile([P, 2, N], F32, name="acc01")
         acc2 = psum.tile([P, N], F32, name="acc2")
         acc3 = [psum.tile([P, P], F32, name="acc3%d" % h, tag=["acc30", "rb_all"][h]) for h in range(HALVES)]
-        for group, (planes, copy) in enumerate(zip(X_GROUPS, [nc.scalar.copy, nc.scalar.copy, nc.scalar.copy])):
-            x_turned = psum.tile([P, len(planes), 2, P], F32, name="x_turned%d" % group, tag="turned%d" % ((group + 1) % 2))
+        for group, (planes, copy) in enumerate(zip(X_GROUPS, [nc.vector.tensor_copy, nc.vector.tensor_copy, nc.scalar.copy, nc.scalar.copy])):
+            x_turned = psum.tile([P, len(planes), 2, P], F32, name="x_turned%d" % group, tag="turned%d" % (group % 2))
             for a, t in enumerate(planes):
                 picked = gather("x_picked%d" % t, x_win[t], x_list, X_GATHER[t])
                 rounded = keep.tile([P, 2, 2 * P], BF16, name="x_rounded%d" % t, align_bytes=64)
@@ -126,7 +125,9 @@ def tile_list_moment_headpicks_bounded_larger_pl_kernel(tc, xf, ra, gt, rb, cp, 
                         ALU.mult,
                     )
                 turn(rounded, x_turned[:, a, :, :])
-            x_words, x_scales = quantise("x%d" % group, x_turned, len(planes), copy)
+            x_words = keep.tile([P, len(planes) * P], U32, name="x_words%d" % group, align_bytes=64)
+            x_scales = keep.tile([P, len(planes) * P], U8, name="x_scales%d" % group, align_bytes=64)
+            quantise("x%d" % group, x_turned, len(planes), copy, x_words[:], x_scales[:])
             for a, t in enumerate(planes):
                 mine = slice(a * P, (a + 1) * P)
                 if t < 3:
@@ -158,7 +159,7 @@ def tile_list_moment_headpicks_bounded_larger_pl_kernel(tc, xf, ra, gt, rb, cp, 
         for h in range(HALVES):
             cols = slice(h * P, (h + 1) * P)
             nc.vector.tensor_tensor(larger[:, 3, cols], acc3[h][:], old_sb[:, 3, cols], ALU.max)
-        for rows in (slice(0, 2), slice(2, PACK)):
+        for rows in (slice(0, 2), slice(2, 3), slice(3, PACK)):
             nc.scalar.activation(y[:, rows, :], larger[:, rows, :], COPY, scale=GAIN)
             nc.sync.dma_start(y_rows[:, rows, :], y[:, rows, :])
         for h in range(HALVES):

@@ -19,12 +19,15 @@ ALU = mybir.AluOpType
 
 P = 128
 PACK = 4
+PAIRS = 2
 HALVES = N // P
+LAST = PACK - 1
+ENTRIES = 16
+QUADRANTS, SCALE_ROWS = 4, 4
+MX_ALIGN = 64
 GAIN = 0.04
-X_GATHER = [[["S",0,512]],[["S",0,512]],[["S",0,512]],[["S",0,256],["S",256,512]]]
-G_GATHER = [[["S",0,512]],[["S",0,512]]]
-X_MULT = [[[0,512]],[[0,512]],[[0,512]],[[0,256],[256,512]]]
-X_GROUPS = [[0],[1],[2],[3]]
+G_SCALAR_SLOTS = (256, 384)
+VECTOR_PLANES = 2
 
 
 def tile_list_moment_headpicks_bounded_larger_pl_kernel(tc, xf, ra, gt, rb, cp, old, offs, offs2, out_0, out_1, out_2):
@@ -33,8 +36,8 @@ def tile_list_moment_headpicks_bounded_larger_pl_kernel(tc, xf, ra, gt, rb, cp, 
         keep = ctx.enter_context(tc.tile_pool(name="keep", bufs=1))
         psum = ctx.enter_context(tc.psum_pool(name="psum", bufs=1))
 
-        x_list = keep.tile([P, J // 16], U16, name="x_list")
-        g_list = keep.tile([P, J // 16], U16, name="g_list")
+        x_list = keep.tile([P, J // ENTRIES], U16, name="x_list")
+        g_list = keep.tile([P, J // ENTRIES], U16, name="g_list")
         x_win = [keep.tile([P, T], F32, name="x_win%d" % t) for t in range(PACK)]
         g_win = [keep.tile([P, V], F32, name="g_win%d" % h) for h in range(HALVES)]
         ra4 = keep.tile([P, PACK], F32, name="ra4")
@@ -52,9 +55,8 @@ def tile_list_moment_headpicks_bounded_larger_pl_kernel(tc, xf, ra, gt, rb, cp, 
         nc.sync.dma_start(bound[1][:], cp[P : 2 * P, :])
         nc.sync.dma_start(x_win[0][:], x_rows[:, 0, :])
         nc.sync.dma_start(x_list[:], offs)
-        nc.sync.dma_start(x_win[1][:], x_rows[:, 1, :])
-        nc.sync.dma_start(x_win[2][:], x_rows[:, 2, :])
-        nc.sync.dma_start(x_win[3][:], x_rows[:, 3, :])
+        for t in range(1, PACK):
+            nc.sync.dma_start(x_win[t][:], x_rows[:, t, :])
         nc.sync.dma_start(old_sb[:], old.rearrange("(p t) n -> p t n", t=PACK))
 
         ident = keep.tile([P, P], F32, name="ident")
@@ -63,114 +65,116 @@ def tile_list_moment_headpicks_bounded_larger_pl_kernel(tc, xf, ra, gt, rb, cp, 
         nc.scalar.activation(ident[:], zero[:].to_broadcast([P, P]), COPY)
         make_identity(nc, ident[:], nomemset=True)
 
-        def spread(name, column4):
+        def spread(name, weights4):
             everywhere = psum.tile([P, PACK, P], F32, name=name)
             for i in range(PACK):
-                nc.tensor.transpose(everywhere[:, i, :], column4[:, i : i + 1].to_broadcast([P, P]), ident[:])
+                nc.tensor.transpose(everywhere[:, i, :], weights4[:, i : i + 1].to_broadcast([P, P]), ident[:])
             return everywhere
 
-        def gather(name, window, offsets, pieces):
-            picked = keep.tile([P, J], F32, name=name)
-            for engine, first, last in pieces:
-                listed = window[:].indirect(offsets[:, first // 16 : last // 16])
-                if engine == "S":
-                    nc.scalar.activation(picked[:, first:last], listed, COPY)
-                else:
-                    nc.vector.tensor_copy(picked[:, first:last], listed)
-            return picked[:].rearrange("p (q u e) -> p u q e", u=2, e=2)
+        def listed(window, offsets, slots):
+            return window[:].indirect(offsets[:, slots.start // ENTRIES : slots.stop // ENTRIES])
 
-        def turn(rounded, turned):
-            for u in range(2):
+        def by_pairs(picked):
+            return picked[:].rearrange("p (q u e) -> p u q e", u=PAIRS, e=2)
+
+        def turn_and_quantise(name, rounded, turned, copy, words, scales):
+            for u in range(PAIRS):
                 nc.tensor.transpose(turned[:, u, :], rounded[:, u, :].bitcast(F32), ident[:])
-
-        def quantise(name, turned, count, copy, words, scales):
-            grouped = keep.tile([P, count * P * PACK], BF16, name=name + "_grouped", align_bytes=64)
-            copy(grouped[:].bitcast(F32).rearrange("q (a c u) -> q a c u", a=count, u=2), turned[:].rearrange("q a u c -> q a c u"))
+            grouped = keep.tile([P, P * PACK], BF16, name=name + "_grouped", align_bytes=MX_ALIGN)
+            copy(grouped[:].bitcast(F32).rearrange("q (c u) -> q c u", u=PAIRS), turned[:].rearrange("q u c -> q c u"))
             nc.vector.quantize_mx(out=words.bitcast(E5M2X4), scales=scales, in_=grouped[:])
 
         rb_all = spread("rb_all", rb4)
-        g_words = keep.tile([P, N], U32, name="g_words", align_bytes=64)
-        g_scales = keep.tile([P, N], U8, name="g_scales", align_bytes=64)
+        g_words = keep.tile([P, N], U32, name="g_words", align_bytes=MX_ALIGN)
+        g_scales = keep.tile([P, N], U8, name="g_scales", align_bytes=MX_ALIGN)
         for h in range(HALVES):
-            g_turned = psum.tile([P, 1, 2, P], F32, name="g_turned%d" % h, tag="turned%d" % h)
-            picked = gather("g_picked%d" % h, g_win[h], g_list, G_GATHER[h])
-            rounded = keep.tile([P, 2, 2 * P], BF16, name="g_rounded%d" % h, align_bytes=64)
-            for u in range(2):
+            turned = psum.tile([P, PAIRS, P], F32, name="g_turned%d" % h, tag="turned%d" % h)
+            picked = keep.tile([P, J], F32, name="g_picked%d" % h)
+            first, rest = slice(0, G_SCALAR_SLOTS[h]), slice(G_SCALAR_SLOTS[h], J)
+            nc.scalar.activation(picked[:, first], listed(g_win[h], g_list, first), COPY)
+            nc.vector.tensor_copy(picked[:, rest], listed(g_win[h], g_list, rest))
+            rounded = keep.tile([P, PAIRS, 2 * P], BF16, name="g_rounded%d" % h, align_bytes=MX_ALIGN)
+            for u in range(PAIRS):
                 nc.vector.scalar_tensor_tensor(
                     rounded[:, u, :].rearrange("p (q e) -> p q e", e=2),
-                    picked[:, u, :, :],
+                    by_pairs(picked)[:, u, :, :],
                     bound[h][:],
                     rb_all[:, 2 * u : 2 * u + 2, :].rearrange("p e q -> p q e"),
                     ALU.min,
                     ALU.mult,
                 )
-            turn(rounded, g_turned[:, 0, :, :])
-            quantise("g%d" % h, g_turned, 1, nc.vector.tensor_copy, g_words[:, h * P : (h + 1) * P], g_scales[:, h * P : (h + 1) * P])
+            cols = slice(h * P, (h + 1) * P)
+            turn_and_quantise("g%d" % h, rounded, turned, nc.vector.tensor_copy, g_words[:, cols], g_scales[:, cols])
 
         ra_all = spread("ra_all", ra4)
         acc01 = psum.tile([P, 2, N], F32, name="acc01")
         acc2 = psum.tile([P, N], F32, name="acc2")
-        acc3 = [psum.tile([P, P], F32, name="acc3%d" % h, tag=["acc30", "rb_all"][h]) for h in range(HALVES)]
-        for group, (planes, copy) in enumerate(zip(X_GROUPS, [nc.vector.tensor_copy, nc.vector.tensor_copy, nc.scalar.copy, nc.scalar.copy])):
-            x_turned = psum.tile([P, len(planes), 2, P], F32, name="x_turned%d" % group, tag="turned%d" % (group % 2))
-            for a, t in enumerate(planes):
-                picked = gather("x_picked%d" % t, x_win[t], x_list, X_GATHER[t])
-                rounded = keep.tile([P, 2, 2 * P], BF16, name="x_rounded%d" % t, align_bytes=64)
-                for first, last in X_MULT[t]:
-                    part = slice(first // PACK, last // PACK)
-                    nc.vector.tensor_tensor(
-                        rounded[:].rearrange("p u (q e) -> p u q e", e=2)[:, :, part, :],
-                        picked[:, :, part, :],
-                        ra_all[:, :, part].rearrange("p (u e) q -> p u q e", e=2),
-                        ALU.mult,
-                    )
-                turn(rounded, x_turned[:, a, :, :])
-            x_words = keep.tile([P, len(planes) * P], U32, name="x_words%d" % group, align_bytes=64)
-            x_scales = keep.tile([P, len(planes) * P], U8, name="x_scales%d" % group, align_bytes=64)
-            quantise("x%d" % group, x_turned, len(planes), copy, x_words[:], x_scales[:])
-            for a, t in enumerate(planes):
-                mine = slice(a * P, (a + 1) * P)
-                if t < 3:
-                    targets = [(acc01[:, t, :] if t < 2 else acc2[:], slice(0, N))]
-                else:
-                    targets = [(acc3[h][:], slice(h * P, (h + 1) * P)) for h in range(HALVES)]
-                for target, cols in targets:
-                    nc.tensor.matmul_mx(
-                        out=target,
-                        lhsT=x_words[:, mine].bitcast(E5M2X4),
-                        lhsT_scale=x_scales[:, mine],
-                        rhs=g_words[:, cols].bitcast(E5M2X4),
-                        rhs_scale=g_scales[:, cols],
-                        start=True,
-                        stop=True,
-                    )
+        acc3 = [psum.tile([P, P], F32, name="acc3%d" % h, tag=("acc30", "rb_all")[h]) for h in range(HALVES)]
+        targets = [
+            [(acc01[:, 0, :], slice(0, N))],
+            [(acc01[:, 1, :], slice(0, N))],
+            [(acc2[:], slice(0, N))],
+            [(acc3[h][:], slice(h * P, (h + 1) * P)) for h in range(HALVES)],
+        ]
+        for t in range(PACK):
+            runs = [slice(0, J // 2), slice(J // 2, J)] if t == LAST else [slice(0, J)]
+            turned = psum.tile([P, PAIRS, P], F32, name="x_turned%d" % t, tag="turned%d" % (t % 2))
+            picked = keep.tile([P, J], F32, name="x_picked%d" % t)
+            for slots in runs:
+                nc.scalar.activation(picked[:, slots], listed(x_win[t], x_list, slots), COPY)
+            rounded = keep.tile([P, PAIRS, 2 * P], BF16, name="x_rounded%d" % t, align_bytes=MX_ALIGN)
+            for slots in runs:
+                quads = slice(slots.start // PACK, slots.stop // PACK)
+                nc.vector.tensor_tensor(
+                    rounded[:].rearrange("p u (q e) -> p u q e", e=2)[:, :, quads, :],
+                    by_pairs(picked)[:, :, quads, :],
+                    ra_all[:, :, quads].rearrange("p (u e) q -> p u q e", e=2),
+                    ALU.mult,
+                )
+            x_words = keep.tile([P, P], U32, name="x_words%d" % t, align_bytes=MX_ALIGN)
+            x_scales = keep.tile([P, P], U8, name="x_scales%d" % t, align_bytes=MX_ALIGN)
+            copy = nc.vector.tensor_copy if t < VECTOR_PLANES else nc.scalar.copy
+            turn_and_quantise("x%d" % t, rounded, turned, copy, x_words[:], x_scales[:])
+            for target, cols in targets[t]:
+                nc.tensor.matmul_mx(
+                    out=target,
+                    lhsT=x_words[:].bitcast(E5M2X4),
+                    lhsT_scale=x_scales[:],
+                    rhs=g_words[:, cols].bitcast(E5M2X4),
+                    rhs_scale=g_scales[:, cols],
+                    start=True,
+                    stop=True,
+                )
 
         y_rows = out_0.rearrange("(p t) n -> p t n", t=PACK)
         word_rows = out_1.rearrange("z p c r -> p (z c r)").bitcast(I32)
         scale_rows = out_2.rearrange("z q c -> q (z c)").bitcast(I32)
         larger = keep.tile([P, PACK, N], F32, name="larger")
         y = keep.tile([P, PACK, N], F32, name="y")
-        y_words = keep.tile([P, N], U32, name="y_words", align_bytes=64)
-        y_scales = keep.tile([P, N], U8, name="y_scales", align_bytes=64)
-        y_grouped = keep.tile([P, N, PACK], BF16, name="y_grouped", align_bytes=64)
+        y_words = keep.tile([P, N], U32, name="y_words", align_bytes=MX_ALIGN)
+        y_scales = keep.tile([P, N], U8, name="y_scales", align_bytes=MX_ALIGN)
+        y_grouped = keep.tile([P, N, PACK], BF16, name="y_grouped", align_bytes=MX_ALIGN)
+        halves = [slice(h * P, (h + 1) * P) for h in range(HALVES)]
         nc.vector.tensor_tensor(larger[:, 0:2, :], acc01[:], old_sb[:, 0:2, :], ALU.max)
-
         nc.vector.tensor_tensor(larger[:, 2, :], acc2[:], old_sb[:, 2, :], ALU.max)
-        for h in range(HALVES):
-            cols = slice(h * P, (h + 1) * P)
-            nc.vector.tensor_tensor(larger[:, 3, cols], acc3[h][:], old_sb[:, 3, cols], ALU.max)
-        for rows in (slice(0, 2), slice(2, 3), slice(3, PACK)):
-            nc.scalar.activation(y[:, rows, :], larger[:, rows, :], COPY, scale=GAIN)
-            nc.sync.dma_start(y_rows[:, rows, :], y[:, rows, :])
-        for h in range(HALVES):
-            cols = slice(h * P, (h + 1) * P)
-            nc.vector.tensor_scalar(y_grouped[:, cols, 0:PACK], larger[:, 0:PACK, cols].rearrange("p t c -> p c t"), GAIN, None, ALU.mult)
-        for h in range(HALVES):
-            cols = slice(h * P, (h + 1) * P)
+        for h, cols in enumerate(halves):
+            nc.vector.tensor_tensor(larger[:, LAST, cols], acc3[h][:], old_sb[:, LAST, cols], ALU.max)
+        for planes in (slice(0, 2), slice(2, LAST), slice(LAST, PACK)):
+            nc.scalar.activation(y[:, planes, :], larger[:, planes, :], COPY, scale=GAIN)
+            nc.sync.dma_start(y_rows[:, planes, :], y[:, planes, :])
+        for cols in halves:
+            nc.vector.tensor_scalar(y_grouped[:, cols, :], larger[:, :, cols].rearrange("p t c -> p c t"), GAIN, None, ALU.mult)
+        for cols in halves:
             nc.vector.quantize_mx(
-                out=y_words[:, cols].bitcast(E4M3X4), scales=y_scales[:, cols], in_=y_grouped[:, cols, :].rearrange("p c t -> p (c t)")
+                out=y_words[:, cols].bitcast(E4M3X4),
+                scales=y_scales[:, cols],
+                in_=y_grouped[:, cols, :].rearrange("p c t -> p (c t)"),
             )
+
         nc.sync.dma_start(word_rows, y_words[:].bitcast(I32))
-        for quad in range(4):
+        for quad in range(QUADRANTS):
             queue = nc.scalar if quad % 2 == 0 else nc.sync
-            queue.dma_start(scale_rows[4 * quad : 4 * quad + 4, :], y_scales[32 * quad : 32 * quad + 4, :].bitcast(I32))
+            queue.dma_start(
+                scale_rows[SCALE_ROWS * quad : SCALE_ROWS * (quad + 1), :],
+                y_scales[32 * quad : 32 * quad + SCALE_ROWS, :].bitcast(I32),
+            )

from contextlib import ExitStack

import concourse.mybir as mybir
from concourse.masks import make_identity

K, J, N, T, V = 512, 512, 256, 1024, 1024
FLOPS = 2 * K * J * N

F32 = mybir.dt.float32
BF16 = mybir.dt.bfloat16
I32 = mybir.dt.int32
U32 = mybir.dt.uint32
U16 = mybir.dt.uint16
U8 = mybir.dt.uint8
E5M2X4 = mybir.dt.float8_e5m2_x4
E4M3X4 = mybir.dt.float8_e4m3fn_x4
COPY = mybir.ActivationFunctionType.Copy
ALU = mybir.AluOpType

P = 128
PACK = 4
PAIRS = 2
HALVES = N // P
LAST = PACK - 1
ENTRIES = 16
QUADRANTS, SCALE_ROWS = 4, 4
MX_ALIGN = 64
GAIN = 0.04
G_SCALAR_SLOTS = (256, 384)
VECTOR_PLANES = 2


def tile_list_moment_headpicks_bounded_larger_pl_kernel(tc, xf, ra, gt, rb, cp, old, offs, offs2, out_0, out_1, out_2):
    nc = tc.nc
    with ExitStack() as ctx:
        keep = ctx.enter_context(tc.tile_pool(name="keep", bufs=1))
        psum = ctx.enter_context(tc.psum_pool(name="psum", bufs=1))

        x_list = keep.tile([P, J // ENTRIES], U16, name="x_list")
        g_list = keep.tile([P, J // ENTRIES], U16, name="g_list")
        x_win = [keep.tile([P, T], F32, name="x_win%d" % t) for t in range(PACK)]
        g_win = [keep.tile([P, V], F32, name="g_win%d" % h) for h in range(HALVES)]
        ra4 = keep.tile([P, PACK], F32, name="ra4")
        rb4 = keep.tile([P, PACK], F32, name="rb4")
        bound = [keep.tile([P, 1], F32, name="bound%d" % h) for h in range(HALVES)]
        old_sb = keep.tile([P, PACK, N], F32, name="old_sb")
        x_rows = xf.rearrange("(p t) c -> p t c", t=PACK)

        nc.sync.dma_start(g_win[0][:], gt[0:P, :])
        nc.sync.dma_start(g_list[:], offs2)
        nc.scalar.dma_start(rb4[:], rb.rearrange("o (q i) -> q (o i)", i=PACK))
        nc.scalar.dma_start(bound[0][:], cp[0:P, :])
        nc.scalar.dma_start(ra4[:], ra.rearrange("o (q i) -> q (o i)", i=PACK))
        nc.sync.dma_start(g_win[1][:], gt[P : 2 * P, :])
        nc.sync.dma_start(bound[1][:], cp[P : 2 * P, :])
        nc.sync.dma_start(x_win[0][:], x_rows[:, 0, :])
        nc.sync.dma_start(x_list[:], offs)
        for t in range(1, PACK):
            nc.sync.dma_start(x_win[t][:], x_rows[:, t, :])
        nc.sync.dma_start(old_sb[:], old.rearrange("(p t) n -> p t n", t=PACK))

        ident = keep.tile([P, P], F32, name="ident")
        zero = keep.tile([P, 1], F32, name="zero")
        nc.gpsimd.memset(zero[:], 0.0)
        nc.scalar.activation(ident[:], zero[:].to_broadcast([P, P]), COPY)
        make_identity(nc, ident[:], nomemset=True)

        def spread(name, weights4):
            everywhere = psum.tile([P, PACK, P], F32, name=name)
            for i in range(PACK):
                nc.tensor.transpose(everywhere[:, i, :], weights4[:, i : i + 1].to_broadcast([P, P]), ident[:])
            return everywhere

        def listed(window, offsets, slots):
            return window[:].indirect(offsets[:, slots.start // ENTRIES : slots.stop // ENTRIES])

        def by_pairs(picked):
            return picked[:].rearrange("p (q u e) -> p u q e", u=PAIRS, e=2)

        def turn_and_quantise(name, rounded, turned, copy, words, scales):
            for u in range(PAIRS):
                nc.tensor.transpose(turned[:, u, :], rounded[:, u, :].bitcast(F32), ident[:])
            grouped = keep.tile([P, P * PACK], BF16, name=name + "_grouped", align_bytes=MX_ALIGN)
            copy(grouped[:].bitcast(F32).rearrange("q (c u) -> q c u", u=PAIRS), turned[:].rearrange("q u c -> q c u"))
            nc.vector.quantize_mx(out=words.bitcast(E5M2X4), scales=scales, in_=grouped[:])

        rb_all = spread("rb_all", rb4)
        g_words = keep.tile([P, N], U32, name="g_words", align_bytes=MX_ALIGN)
        g_scales = keep.tile([P, N], U8, name="g_scales", align_bytes=MX_ALIGN)
        for h in range(HALVES):
            turned = psum.tile([P, PAIRS, P], F32, name="g_turned%d" % h, tag="turned%d" % h)
            picked = keep.tile([P, J], F32, name="g_picked%d" % h)
            first, rest = slice(0, G_SCALAR_SLOTS[h]), slice(G_SCALAR_SLOTS[h], J)
            nc.scalar.activation(picked[:, first], listed(g_win[h], g_list, first), COPY)
            nc.vector.tensor_copy(picked[:, rest], listed(g_win[h], g_list, rest))
            rounded = keep.tile([P, PAIRS, 2 * P], BF16, name="g_rounded%d" % h, align_bytes=MX_ALIGN)
            for u in range(PAIRS):
                nc.vector.scalar_tensor_tensor(
                    rounded[:, u, :].rearrange("p (q e) -> p q e", e=2),
                    by_pairs(picked)[:, u, :, :],
                    bound[h][:],
                    rb_all[:, 2 * u : 2 * u + 2, :].rearrange("p e q -> p q e"),
                    ALU.min,
                    ALU.mult,
                )
            cols = slice(h * P, (h + 1) * P)
            turn_and_quantise("g%d" % h, rounded, turned, nc.vector.tensor_copy, g_words[:, cols], g_scales[:, cols])

        ra_all = spread("ra_all", ra4)
        acc01 = psum.tile([P, 2, N], F32, name="acc01")
        acc2 = psum.tile([P, N], F32, name="acc2")
        acc3 = [psum.tile([P, P], F32, name="acc3%d" % h, tag=("acc30", "rb_all")[h]) for h in range(HALVES)]
        targets = [
            [(acc01[:, 0, :], slice(0, N))],
            [(acc01[:, 1, :], slice(0, N))],
            [(acc2[:], slice(0, N))],
            [(acc3[h][:], slice(h * P, (h + 1) * P)) for h in range(HALVES)],
        ]
        for t in range(PACK):
            runs = [slice(0, J // 2), slice(J // 2, J)] if t == LAST else [slice(0, J)]
            turned = psum.tile([P, PAIRS, P], F32, name="x_turned%d" % t, tag="turned%d" % (t % 2))
            picked = keep.tile([P, J], F32, name="x_picked%d" % t)
            for slots in runs:
                nc.scalar.activation(picked[:, slots], listed(x_win[t], x_list, slots), COPY)
            rounded = keep.tile([P, PAIRS, 2 * P], BF16, name="x_rounded%d" % t, align_bytes=MX_ALIGN)
            for slots in runs:
                quads = slice(slots.start // PACK, slots.stop // PACK)
                nc.vector.tensor_tensor(
                    rounded[:].rearrange("p u (q e) -> p u q e", e=2)[:, :, quads, :],
                    by_pairs(picked)[:, :, quads, :],
                    ra_all[:, :, quads].rearrange("p (u e) q -> p u q e", e=2),
                    ALU.mult,
                )
            x_words = keep.tile([P, P], U32, name="x_words%d" % t, align_bytes=MX_ALIGN)
            x_scales = keep.tile([P, P], U8, name="x_scales%d" % t, align_bytes=MX_ALIGN)
            copy = nc.vector.tensor_copy if t < VECTOR_PLANES else nc.scalar.copy
            turn_and_quantise("x%d" % t, rounded, turned, copy, x_words[:], x_scales[:])
            for target, cols in targets[t]:
                nc.tensor.matmul_mx(
                    out=target,
                    lhsT=x_words[:].bitcast(E5M2X4),
                    lhsT_scale=x_scales[:],
                    rhs=g_words[:, cols].bitcast(E5M2X4),
                    rhs_scale=g_scales[:, cols],
                    start=True,
                    stop=True,
                )

        y_rows = out_0.rearrange("(p t) n -> p t n", t=PACK)
        word_rows = out_1.rearrange("z p c r -> p (z c r)").bitcast(I32)
        scale_rows = out_2.rearrange("z q c -> q (z c)").bitcast(I32)
        larger = keep.tile([P, PACK, N], F32, name="larger")
        y = keep.tile([P, PACK, N], F32, name="y")
        y_words = keep.tile([P, N], U32, name="y_words", align_bytes=MX_ALIGN)
        y_scales = keep.tile([P, N], U8, name="y_scales", align_bytes=MX_ALIGN)
        y_grouped = keep.tile([P, N, PACK], BF16, name="y_grouped", align_bytes=MX_ALIGN)
        halves = [slice(h * P, (h + 1) * P) for h in range(HALVES)]
        nc.vector.tensor_tensor(larger[:, 0:2, :], acc01[:], old_sb[:, 0:2, :], ALU.max)
        nc.vector.tensor_tensor(larger[:, 2, :], acc2[:], old_sb[:, 2, :], ALU.max)
        for h, cols in enumerate(halves):
            nc.vector.tensor_tensor(larger[:, LAST, cols], acc3[h][:], old_sb[:, LAST, cols], ALU.max)
        for planes in (slice(0, 2), slice(2, LAST), slice(LAST, PACK)):
            nc.scalar.activation(y[:, planes, :], larger[:, planes, :], COPY, scale=GAIN)
            nc.sync.dma_start(y_rows[:, planes, :], y[:, planes, :])
        for cols in halves:
            nc.vector.tensor_scalar(y_grouped[:, cols, :], larger[:, :, cols].rearrange("p t c -> p c t"), GAIN, None, ALU.mult)
        for cols in halves:
            nc.vector.quantize_mx(
                out=y_words[:, cols].bitcast(E4M3X4),
                scales=y_scales[:, cols],
                in_=y_grouped[:, cols, :].rearrange("p c t -> p (c t)"),
            )

        nc.sync.dma_start(word_rows, y_words[:].bitcast(I32))
        for quad in range(QUADRANTS):
            queue = nc.scalar if quad % 2 == 0 else nc.sync
            queue.dma_start(
                scale_rows[SCALE_ROWS * quad : SCALE_ROWS * (quad + 1), :],
                y_scales[32 * quad : 32 * quad + SCALE_ROWS, :].bitcast(I32),
            )
